import numpy as np
import ml_dtypes


def mxq(x, axis, fmt="e4m3"):
    dtype, down = {"e4m3": (ml_dtypes.float8_e4m3fn, 7), "e5m2": (ml_dtypes.float8_e5m2, 14)}[fmt]
    v = np.moveaxis(np.asarray(x, np.float32).astype(ml_dtypes.bfloat16).astype(np.float64), axis, -1)
    blocks = v.reshape(v.shape[:-1] + (-1, 32))
    amax = np.abs(blocks).max(-1, keepdims=True)
    byte = np.maximum(np.where(amax > 0, np.frexp(amax)[1] - 1 + 127, 0) - down, 1)
    scale = np.exp2(byte - 127.0)
    codes = (blocks / scale).astype(np.float32).astype(dtype).astype(np.float64)
    return np.moveaxis((codes * scale).reshape(v.shape), -1, axis)


WIDE = False


def mx_kscale(k):
    if not WIDE:
        return np.ones(k)
    levels = np.array([10, -10, 5, -5, 0])
    if k % 512:
        return np.exp2(np.random.permutation(np.resize(levels, k // 32))).repeat(32)
    a = np.empty((k // 512, 16))
    for p in range(k // 512):
        a[p, :8] = np.random.permutation(np.resize(levels, 8))
        for g in range(8):
            far = levels[np.abs(levels - a[p, g]) >= 10]
            a[p, g + 8] = far[np.random.randint(len(far))]
    return np.exp2(a.ravel()).repeat(32)


def f64(x):
    return np.asarray(x).astype(np.float64)


def striped(idx):
    return np.tile(idx.reshape(-1, 16).T, (8, 1)).astype(np.uint16)


def unstriped(offs):
    return offs[:16].T.reshape(-1).astype(np.int64)


def striped8(idx):
    return np.concatenate([x.reshape(-1, 16).T for x in idx]).astype(np.uint16)


def runs(offs, k):
    lists = np.stack([offs[16 * r : 16 * r + 16].T.reshape(-1) for r in range(8)]).astype(np.int64)
    return lists[np.arange(k) % 512 // 64]


def pack_weight(w):
    k, n = w.shape
    w = f64(np.asarray(w, np.float32).astype(ml_dtypes.bfloat16)).reshape(k // 32, 32, n)
    amax = np.abs(w).max(1)
    byte = np.clip(np.where(amax > 0, np.frexp(amax)[1] - 1 + 127 - 7, 1), 1, 254)
    scaled = (w * np.exp2(127.0 - byte)[:, None, :]).reshape(k, n).astype(np.float32)
    words = np.ascontiguousarray(scaled.reshape(k // 512, 128, 4, n).transpose(0, 1, 3, 2)).astype(ml_dtypes.float8_e4m3fn).view(np.uint8)
    return words, np.ascontiguousarray(byte.astype(np.uint8).reshape(k // 512, 16, n))


def unpack_weight(words, scales):
    g, p, n, _ = words.shape
    vals = np.ascontiguousarray(words).view(ml_dtypes.float8_e4m3fn).astype(np.float64) * np.repeat(np.exp2(scales.astype(np.float64) - 127.0), 8, axis=1)[..., None]
    return vals.transpose(0, 1, 3, 2).reshape(g * 512, n)


E2M1 = np.array([0.0, 0.5, 1.0, 1.5, 2.0, 3.0, 4.0, 6.0, -0.0, -0.5, -1.0, -1.5, -2.0, -3.0, -4.0, -6.0])


def pack_fp4(w):
    k, n = w.shape
    w = f64(np.asarray(w, np.float32).astype(ml_dtypes.bfloat16)).reshape(k // 32, 32, n)
    amax = np.abs(w).max(1)
    mant, ex = np.frexp(amax / 6.0)
    byte = np.clip(np.where(amax > 0, np.where(mant > 0.5, ex, ex - 1) + 127, 1), 1, 254)
    scaled = (w * np.exp2(127.0 - byte)[:, None, :]).reshape(k, n).astype(np.float32)
    c = np.ascontiguousarray(scaled.reshape(k // 512, 128, 4, n).transpose(0, 1, 3, 2)).astype(ml_dtypes.float4_e2m1fn).view(np.uint8) & 0xF
    words = (c[..., 0::2] | (c[..., 1::2] << 4)).reshape(k // 512, 128, 2 * n)
    return np.ascontiguousarray(words), np.ascontiguousarray(byte.astype(np.uint8).reshape(k // 512, 16, n))


def unpack_fp4(words, scales):
    g, _, n = scales.shape
    words = np.ascontiguousarray(words).reshape(g, 128, n, 2)
    nib = np.empty((g, 128, n, 4), np.uint8)
    nib[..., 0::2] = words & 0xF
    nib[..., 1::2] = words >> 4
    vals = E2M1[nib] * np.repeat(np.exp2(scales.astype(np.float64) - 127.0), 8, axis=1)[..., None]
    return vals.transpose(0, 1, 3, 2).reshape(g * 512, n)


def sigmoid(v):
    return 1.0 / (1.0 + np.exp(-np.maximum(v, -700.0)))

def planes(y):
    n, m = y.shape
    v = y.astype(np.float32).astype(ml_dtypes.bfloat16).astype(np.float64).reshape(n // 32, 32, m)
    top = np.abs(v).max(1)
    byte = np.clip(np.where(top > 0, np.frexp(top)[1] - 1 + 127 - 7, 1), 1, 254)
    codes = (v * np.exp2(127.0 - byte)[:, None, :]).reshape(n, m).astype(np.float32).astype(ml_dtypes.float8_e4m3fn).view(np.uint8)
    words = codes.reshape(n // 512, 128, 4, m).transpose(0, 1, 3, 2)
    return np.ascontiguousarray(words), np.ascontiguousarray(byte.astype(np.uint8).reshape(n // 512, 16, m))


K, T, S, N, G, H = 512, 1024, 512, 512, 2048, 512


def setup_inputs():
    n = np.random.standard_normal
    s = mx_kscale(K)[:, None]
    u = mx_kscale(S)
    packed_xT = pack_weight(n((K, T)) * s)
    packed_dT = pack_weight(n((K, G)) / s)
    packed_w1 = pack_fp4(n((H, N)) / np.sqrt(H) / u[:, None])
    return {
        "x_words": packed_xT[0],
        "x_scales": packed_xT[1],
        "d_words": packed_dT[0],
        "d_scales": packed_dT[1],
        "gn": (np.random.uniform(0.5, 1.5, (H, 1)) * u[:, None]).astype(np.float32),
        "w1_words": packed_w1[0],
        "w1_scales": packed_w1[1],
        "offs": striped(np.random.permutation(T)[:S]),
        "k1": striped8(np.random.randint(0, G, (8, H))),
        "two": striped(np.random.permutation(T)[:S]),
        "k2": striped8(np.random.randint(0, G, (8, H))),
        "n1": striped(np.random.permutation(S)),
        "n2": striped(np.random.permutation(S)),
        "n3": striped(np.random.permutation(S)),
        "n4": striped(np.random.permutation(S)),
    }


def reference(x_words, x_scales, d_words, d_scales, gn, w1_words, w1_scales, offs, k1, two, k2, n1, n2, n3, n4):
    d_k1 = unpack_weight(d_words, d_scales)[np.arange(K)[:, None], runs(k1, K)]
    xq = unpack_weight(x_words, x_scales)[:, unstriped(offs)]
    a = 0.0625 * (d_k1.T @ xq)
    d_k2 = unpack_weight(d_words, d_scales)[np.arange(K)[:, None], runs(k2, K)]
    x_two = unpack_weight(x_words, x_scales)[:, unstriped(two)]
    b = 0.0625 * (d_k2.T @ x_two)
    z = f64(gn) * (a + (sigmoid(b[:, unstriped(n2)] - b)) * (a[:, unstriped(n1)] - a))
    h = unpack_fp4(w1_words, w1_scales).T @ mxq(z, 0, "e4m3")
    out_0 = h[:, unstriped(n3)] / (np.abs(h) + np.abs(h[:, unstriped(n4)]) + 0.5)
    return (out_0,) + planes(out_0)

@@ -1,0 +1,259 @@
+from contextlib import ExitStack
+
+import concourse.mybir as mybir
+
+F32 = mybir.dt.float32
+BF16 = mybir.dt.bfloat16
+I32 = mybir.dt.int32
+U32 = mybir.dt.uint32
+U16 = mybir.dt.uint16
+U8 = mybir.dt.uint8
+FP8X4 = mybir.dt.float8_e4m3fn_x4
+FP4X4 = mybir.dt.float4_e2m1fn_x4
+ACT = mybir.ActivationFunctionType
+ALU = mybir.AluOpType
+
+P = 128
+PACK = 4
+S = 512
+T = 1024
+G = 2048
+HALF = S // 2
+LIST_COLS = S // 16
+FLOPS = 3 * 2 * 512 * 512 * 512
+
+
+def tile_picked_twpqpullbnorm2_none_po_kernel(
+    tc, x_words, x_scales, d_words, d_scales, gn, w1_words, w1_scales,
+    offs, k1, two, k2, n1, n2, n3, n4, out_0, out_1, out_2,
+):
+    nc = tc.nc
+    with ExitStack() as ctx:
+        lists = ctx.enter_context(tc.tile_pool(name="lists", bufs=1))
+        sb = ctx.enter_context(tc.tile_pool(name="sb", bufs=1))
+        psum = ctx.enter_context(tc.psum_pool(name="psum", bufs=1))
+
+        def load_list(src, name):
+            dst = lists.tile([P, LIST_COLS], U16, name=name)
+            nc.sync.dma_start(dst[:], src)
+            return dst
+
+        def half_of(lst, h):
+            return lst[:, h * (LIST_COLS // 2) : (h + 1) * (LIST_COLS // 2)]
+
+        def cols(h):
+            return slice(h * HALF, (h + 1) * HALF)
+
+        d_sc = sb.tile([P, G], U8, name="d_sc", align_bytes=64)
+        x_sc = sb.tile([P, T], U8, name="x_sc", align_bytes=64)
+        nc.gpsimd.memset(d_sc[:].bitcast(I32), 0)
+        nc.vector.memset(x_sc[:].bitcast(I32), 0)
+        k2_l = load_list(k2, "k2_l")
+        two_l = load_list(two, "two_l")
+        nc.sync.dma_start(d_sc[0:P:8, :].bitcast(I32), d_scales[0].bitcast(I32))
+        nc.sync.dma_start(x_sc[0:P:8, :].bitcast(I32), x_scales[0].bitcast(I32))
+        x_w = sb.tile([P, T], I32, name="x_w", align_bytes=64)
+        d_w = sb.tile([P, G], I32, name="d_w", align_bytes=64)
+        nc.sync.dma_start(x_w[:], x_words[0].rearrange("p n r -> p (n r)").bitcast(I32))
+        nc.sync.dma_start(d_w[:], d_words[0].rearrange("p n r -> p (n r)").bitcast(I32))
+        k1_l = load_list(k1, "k1_l")
+        offs_l = load_list(offs, "offs_l")
+        gain_raw = sb.tile([P, PACK], F32, name="gain_raw")
+        nc.gpsimd.dma_start(gain_raw[:], gn.rearrange("(p t) o -> p (t o)", t=PACK))
+
+        gain = sb.tile([P, PACK], F32, name="gain")
+        nc.scalar.activation(gain[:], gain_raw[:], ACT.Copy, scale=0.0625 * 0.5)
+
+        def coded_product(d_list, x_list, name, banks, slots):
+            picked_sc = sb.tile([P, 2 * S], U8, name=name + "_picked_sc", tag=slots[0], align_bytes=64)
+            nc.vector.tensor_copy(picked_sc[:, 0:S], d_sc[:].indirect(d_list[:]))
+            nc.vector.tensor_copy(picked_sc[:, S : 2 * S], x_sc[:].indirect(x_list[:]))
+            placed_sc = sb.tile([P, 2 * S], U8, name=name + "_placed_sc", align_bytes=64)
+            nc.vector.tensor_copy(
+                placed_sc[:, 0:S].rearrange("p (t m i) -> p m t i", t=PACK, i=16),
+                picked_sc[:, 0:S].rearrange("p (m i t) -> p m t i", t=PACK, i=16),
+            )
+            nc.vector.tensor_copy(placed_sc[:, S : 2 * S].bitcast(I32), picked_sc[:, S : 2 * S].bitcast(I32))
+            for c in range(1, 4):
+                nc.sync.dma_start(placed_sc[c:P:32, :].bitcast(I32), placed_sc[8 * c : P : 32, :].bitcast(I32))
+            x_pick = sb.tile([P, S], U32, name=name + "_x_pick", tag="x_pick", align_bytes=64)
+            d_pick = sb.tile([P, S], U32, name=name + "_d_pick", tag=slots[1], align_bytes=64)
+            d_dealt = sb.tile([P, S], U32, name=name + "_d_dealt", tag=slots[2], align_bytes=64)
+            picks = [(x_pick, x_w, x_list), (d_pick, d_w, d_list)]
+            for dst, table, lst in picks if name == "b" else picks[::-1]:
+                nc.vector.tensor_copy(dst[:], table[:].bitcast(U32).indirect(lst[:]))
+            nc.vector.tensor_copy(
+                d_dealt[:].rearrange("p (t m i) -> p m t i", t=PACK, i=4),
+                d_pick[:].rearrange("p (m i t) -> p m t i", t=PACK, i=4),
+            )
+            acc = []
+            for t in range(PACK):
+                bank = psum.tile([P, S], F32, name=name + "_acc%d" % t, tag="bank%d" % banks[t])
+                nc.tensor.matmul_mx(
+                    out=bank[:],
+                    lhsT=d_dealt[:, t * P : (t + 1) * P].bitcast(FP8X4),
+                    lhsT_scale=placed_sc[:, t * P : (t + 1) * P],
+                    rhs=x_pick[:].bitcast(FP8X4),
+                    rhs_scale=placed_sc[:, S : 2 * S],
+                    start=True,
+                    stop=True,
+                )
+                acc.append(bank)
+            return acc
+
+        b_acc = coded_product(k2_l, two_l, "b", [0, 1, 2, 3], ["slot0", "slot1", "slot2"])
+
+        n2_l = load_list(n2, "n2_l")
+        n1_l = load_list(n1, "n1_l")
+        n4_l = load_list(n4, "n4_l")
+        n3_l = load_list(n3, "n3_l")
+        w_raw = sb.tile([P, 2 * S], U8, name="w_raw", align_bytes=64)
+        nc.gpsimd.dma_start(w_raw[:].bitcast(I32), w1_words[0].bitcast(I32))
+        w_sc_raw = sb.tile([P, S], U8, name="w_sc_raw", align_bytes=64)
+        nc.gpsimd.memset(w_sc_raw[:].bitcast(I32), 0)
+        for q in range(4):
+            nc.gpsimd.dma_start(w_sc_raw[32 * q : 32 * q + 4, :].bitcast(I32), w1_scales[0, 4 * q : 4 * q + 4, :].bitcast(I32))
+        w_dealt = sb.tile([P, 2 * S], U8, name="w_dealt", align_bytes=64)
+        nc.scalar.copy(
+            w_dealt[:].bitcast(U16).rearrange("p (t m i) -> p m t i", t=PACK, i=8),
+            w_raw[:].bitcast(U16).rearrange("p (m i t) -> p m t i", t=PACK, i=8),
+        )
+        w_sc = sb.tile([P, S], U8, name="w_sc", align_bytes=64)
+        nc.gpsimd.tensor_copy(
+            w_sc[:].rearrange("p (t m i) -> p m t i", t=PACK, i=16),
+            w_sc_raw[:].rearrange("p (m i t) -> p m t i", t=PACK, i=16),
+        )
+        half_bias = sb.tile([P, 1], F32, name="half_bias")
+        nc.gpsimd.memset(half_bias[:], 0.5)
+
+        def entries(lst, span):
+            return lst[:, span.start // 16 : span.stop // 16]
+
+        def spans(widths):
+            return [slice(sum(widths[:n]), sum(widths[: n + 1])) for n in range(len(widths))]
+
+        b_val = [sb.tile([P, S], F32, name="b_val%d" % t) for t in range(PACK)]
+        b_dup = [sb.tile([P, HALF], F32, name="b_dup%d" % t) for t in range(PACK)]
+        for t in range(PACK):
+            nc.scalar.copy(b_val[t][:], b_acc[t][:])
+        b_far = sb.tile([P, PACK, S], F32, name="b_far")
+        for h, rows in ((0, range(PACK)), (1, range(PACK - 2))):
+            for t in rows:
+                nc.scalar.activation(b_far[:, t, cols(h)], b_val[t][:].indirect(half_of(n2_l, h)), ACT.Copy)
+
+        a_acc = coded_product(k1_l, offs_l, "a", [4, 5, 6, 7], ["slot1", "slot2", "slot3"])
+        for t in range(PACK - 2, PACK):
+            nc.sync.dma_start(b_dup[t][:], b_val[t][:, cols(1)])
+        diff = sb.tile([P, PACK, S], F32, name="diff")
+        for t in range(PACK):
+            if t < PACK - 2:
+                nc.vector.tensor_tensor(diff[:, t, :], b_far[:, t, :], b_val[t][:], ALU.subtract)
+            else:
+                nc.vector.tensor_tensor(diff[:, t, cols(0)], b_far[:, t, cols(0)], b_val[t][:, cols(0)], ALU.subtract)
+                nc.vector.tensor_tensor(diff[:, t, cols(1)], b_val[t][:].indirect(half_of(n2_l, 1)), b_dup[t][:], ALU.subtract)
+        a_all = sb.tile([P, PACK, S], F32, name="a_all")
+        th = sb.tile([P, PACK, S], F32, name="th")
+        near = sb.tile([P, PACK, S], F32, name="near")
+        for t in range(PACK):
+            if t < 2:
+                nc.scalar.activation(a_all[:, t, :], a_acc[t][:], ACT.Copy, scale=gain[:, t : t + 1])
+            else:
+                nc.vector.tensor_scalar(a_all[:, t, :], a_acc[t][:], gain[:, t : t + 1], None, ALU.mult)
+            nc.scalar.activation(th[:, t, :], diff[:, t, :], ACT.Tanh, scale=0.0625 * 0.5)
+
+        def near_part(t, span):
+            nc.vector.scalar_tensor_tensor(near[:, t, span], th[:, t, span], 1.0, a_all[:, t, span], ALU.subtract, ALU.mult)
+
+        for t in range(PACK):
+            near_part(t, slice(0, S))
+
+        h_val = [sb.tile([P, S], F32, name="h_val%d" % t) for t in range(PACK)]
+        h_abs = [sb.tile([P, S], F32, name="h_abs%d" % t) for t in range(PACK)]
+        h_dup = [sb.tile([P, S], F32, name="h_dup%d" % t, tag="h_dup%d" % t) for t in range(PACK)]
+        order1 = [cols(0), slice(256,384), slice(384,512)]
+        h_acc = []
+        for n, span in enumerate(order1):
+            w = span.stop - span.start
+            a_far = sb.tile([P, PACK, w], F32, name="a_far%d" % n, tag="a_far%d" % n)
+            for t in range(PACK):
+                nc.scalar.activation(a_far[:, t, :], a_all[:, t, :].indirect(entries(n1_l, span)), ACT.Copy)
+            far = sb.tile([P, PACK, w], F32, name="far%d" % n, tag="a_far%d" % (n - 1))
+            for u in range(2 if n == 0 else 1):
+                k = PACK // (2 if n == 0 else 1)
+                rows = slice(u * k, (u + 1) * k)
+                nc.vector.scalar_tensor_tensor(far[:, rows, :], th[:, rows, span], 1.0, a_far[:, rows, :], ALU.add, ALU.mult)
+            z = sb.tile([P, w * PACK], BF16, name="z%d" % n, align_bytes=64)
+            nc.vector.tensor_tensor(
+                z[:].rearrange("p (c i t) -> p c t i", t=PACK, i=2),
+                far[:].rearrange("p t (c i) -> p c t i", i=2),
+                near[:, :, span].rearrange("p t (c i) -> p c t i", i=2),
+                ALU.subtract,
+            )
+            z_w = sb.tile([P, w], U32, name="z_w%d" % n, align_bytes=64)
+            z_sc = sb.tile([P, w], U8, name="z_sc%d" % n, align_bytes=64)
+            nc.vector.quantize_mx(out=z_w[:].bitcast(FP8X4), scales=z_sc[:], in_=z[:])
+            if n == 0:
+                banks = [psum.tile([P, S], F32, name="h_acc0_%d" % t, tag="bank%d" % t)[:, 0:w] for t in range(PACK)]
+            else:
+                two_banks = [psum.tile([P, S], F32, name="h_acc%d_%d" % (n, u), tag="bank%d" % (2 + 2 * n + u)) for u in range(2)]
+                banks = [two_banks[t // 2][:, (t % 2) * w : (t % 2 + 1) * w] for t in range(PACK)]
+            for t in range(PACK):
+                nc.tensor.matmul_mx(
+                    out=banks[t],
+                    lhsT=w_dealt[:, 2 * t * P : 2 * (t + 1) * P].bitcast(FP4X4),
+                    lhsT_scale=w_sc[:, t * P : (t + 1) * P],
+                    rhs=z_w[:].bitcast(FP8X4),
+                    rhs_scale=z_sc[:],
+                    start=True,
+                    stop=True,
+                )
+            for t in range(PACK):
+                nc.scalar.activation(h_abs[t][:, span], banks[t], ACT.Abs)
+                if n < 3:
+                    nc.sync.dma_start(h_dup[t][:, span], h_abs[t][:, span])
+            h_acc.append(banks)
+            if n in []:
+                for t in range(PACK):
+                    nc.scalar.copy(h_val[t][:, span], banks[t])
+        for n, span in enumerate(order1):
+            w = span.stop - span.start
+            for t in range(PACK):
+                if n in [0, 1]:
+                    nc.vector.tensor_copy(h_val[t][:, span], h_acc[n][t])
+                elif n not in []:
+                    nc.scalar.copy(h_val[t][:, span], h_acc[n][t])
+                if n >= 3:
+                    nc.scalar.copy(h_dup[t][:, span], h_abs[t][:, span])
+
+        o_w = sb.tile([P, S], U32, name="o_w", align_bytes=64)
+        o_sc = sb.tile([P, S], U8, name="o_sc", align_bytes=64)
+        order2 = [cols(0), slice(256,384), slice(384,512)]
+        den = sb.tile([P, PACK, S], F32, name="den")
+        for span in [cols(0), cols(1)]:
+            for t in range(PACK):
+                nc.vector.tensor_tensor(den[:, t, span], h_abs[t][:].indirect(entries(n4_l, span)), h_dup[t][:, span], ALU.add)
+        out_rows = out_0.rearrange("(p t) j -> p t j", t=PACK)
+        out_words = out_1[0].rearrange("p n r -> p (n r)").bitcast(I32)
+        root = sb.tile([P, PACK, S], F32, name="root")
+        inv = sb.tile([P, PACK, S], F32, name="inv")
+        for span in [cols(0), cols(1)]:
+            for u in range(2):
+                pair = slice(2 * u, 2 * u + 2)
+                nc.scalar.activation(root[:, pair, span], den[:, pair, span], ACT.Abs_reciprocal_sqrt, bias=half_bias[:])
+                nc.scalar.activation(inv[:, pair, span], root[:, pair, span], ACT.Square)
+        for n, span in enumerate(order2):
+            w = span.stop - span.start
+            res = sb.tile([P, PACK, w], F32, name="res%d" % n, tag=["h_dup2", "h_dup3", "res2"][n])
+            for t in range(PACK):
+                nc.vector.tensor_tensor(res[:, t, :], h_val[t][:].indirect(entries(n3_l, span)), inv[:, t, span], ALU.mult)
+            nc.sync.dma_start(out_rows[:, :, span], res[:])
+            res_bf = sb.tile([P, w * PACK], BF16, name="res_bf%d" % n, align_bytes=64)
+            rounder = nc.scalar.copy if n < len(order2) - 1 else nc.vector.tensor_copy
+            rounder(
+                res_bf[:].rearrange("p (c i t) -> p c t i", t=PACK, i=2),
+                res[:].rearrange("p t (c i) -> p c t i", i=2),
+            )
+            nc.vector.quantize_mx(out=o_w[:, span].bitcast(FP8X4), scales=o_sc[:, span], in_=res_bf[:])
+            nc.sync.dma_start(out_words[:, span], o_w[:, span].bitcast(I32))
+        for q in range(4):
+            (nc.sync if q < 2 else nc.scalar).dma_start(out_2[0, 4 * q : 4 * q + 4, :].bitcast(I32), o_sc[32 * q : 32 * q + 4, :].bitcast(I32))

@@ -49,9 +49,10 @@ def tile_picked_twpqpullbnorm2_none_po_kernel(
         nc.gpsimd.memset(d_sc[:].bitcast(I32), 0)
         nc.vector.memset(x_sc[:].bitcast(I32), 0)
         k2_l = load_list(k2, "k2_l")
-        two_l = load_list(two, "two_l")
         nc.sync.dma_start(d_sc[0:P:8, :].bitcast(I32), d_scales[0].bitcast(I32))
-        nc.sync.dma_start(x_sc[0:P:8, :].bitcast(I32), x_scales[0].bitcast(I32))
+        two_l = load_list(two, "two_l")
+        for q in range(4):
+            nc.sync.dma_start(x_sc[32 * q : 32 * q + 4, :].bitcast(I32), x_scales[0, 4 * q : 4 * q + 4, :].bitcast(I32))
         x_w = sb.tile([P, T], I32, name="x_w", align_bytes=64)
         d_w = sb.tile([P, G], I32, name="d_w", align_bytes=64)
         nc.sync.dma_start(x_w[:], x_words[0].rearrange("p n r -> p (n r)").bitcast(I32))
@@ -64,44 +65,46 @@ def tile_picked_twpqpullbnorm2_none_po_kernel(
         gain = sb.tile([P, PACK], F32, name="gain")
         nc.scalar.activation(gain[:], gain_raw[:], ACT.Copy, scale=0.0625 * 0.5)
 
-        def coded_product(d_list, x_list, name, banks, slots):
+        def coded_product(d_list, x_list, name, slots):
             picked_sc = sb.tile([P, 2 * S], U8, name=name + "_picked_sc", tag=slots[0], align_bytes=64)
             nc.vector.tensor_copy(picked_sc[:, 0:S], d_sc[:].indirect(d_list[:]))
             nc.vector.tensor_copy(picked_sc[:, S : 2 * S], x_sc[:].indirect(x_list[:]))
-            placed_sc = sb.tile([P, 2 * S], U8, name=name + "_placed_sc", align_bytes=64)
+            placed_sc = sb.tile([P, S], U8, name=name + "_placed_sc", align_bytes=64)
             nc.vector.tensor_copy(
                 placed_sc[:, 0:S].rearrange("p (t m i) -> p m t i", t=PACK, i=16),
                 picked_sc[:, 0:S].rearrange("p (m i t) -> p m t i", t=PACK, i=16),
             )
-            nc.vector.tensor_copy(placed_sc[:, S : 2 * S].bitcast(I32), picked_sc[:, S : 2 * S].bitcast(I32))
             for c in range(1, 4):
                 nc.sync.dma_start(placed_sc[c:P:32, :].bitcast(I32), placed_sc[8 * c : P : 32, :].bitcast(I32))
-            x_pick = sb.tile([P, S], U32, name=name + "_x_pick", tag="x_pick", align_bytes=64)
-            d_pick = sb.tile([P, S], U32, name=name + "_d_pick", tag=slots[1], align_bytes=64)
-            d_dealt = sb.tile([P, S], U32, name=name + "_d_dealt", tag=slots[2], align_bytes=64)
-            picks = [(x_pick, x_w, x_list), (d_pick, d_w, d_list)]
-            for dst, table, lst in picks if name == "b" else picks[::-1]:
-                nc.vector.tensor_copy(dst[:], table[:].bitcast(U32).indirect(lst[:]))
-            nc.vector.tensor_copy(
-                d_dealt[:].rearrange("p (t m i) -> p m t i", t=PACK, i=4),
-                d_pick[:].rearrange("p (m i t) -> p m t i", t=PACK, i=4),
-            )
-            acc = []
-            for t in range(PACK):
-                bank = psum.tile([P, S], F32, name=name + "_acc%d" % t, tag="bank%d" % banks[t])
-                nc.tensor.matmul_mx(
-                    out=bank[:],
-                    lhsT=d_dealt[:, t * P : (t + 1) * P].bitcast(FP8X4),
-                    lhsT_scale=placed_sc[:, t * P : (t + 1) * P],
-                    rhs=x_pick[:].bitcast(FP8X4),
-                    rhs_scale=placed_sc[:, S : 2 * S],
-                    start=True,
-                    stop=True,
+            d_pick = [sb.tile([P, HALF], U32, name=name + "_d_pick%d" % h, tag=slots[3 + h], align_bytes=64) for h in range(2)]
+            x_pick = [sb.tile([P, HALF], U32, name=name + "_x_pick%d" % h, tag=slots[1 + h], align_bytes=64) for h in range(2)]
+            d_dealt = sb.tile([P, S], U32, name=name + "_d_dealt", tag=slots[5], align_bytes=64)
+            nc.vector.tensor_copy(x_pick[0][:], x_w[:].bitcast(U32).indirect(half_of(x_list, 0)))
+            for h in range(2):
+                nc.vector.tensor_copy(d_pick[h][:], d_w[:].bitcast(U32).indirect(half_of(d_list, h)))
+            for h in range(2):
+                nc.vector.tensor_copy(
+                    d_dealt[:].rearrange("p (t h m i) -> p h m t i", t=PACK, h=2, i=4)[:, h],
+                    d_pick[h][:].rearrange("p (m i t) -> p m t i", t=PACK, i=4),
                 )
-                acc.append(bank)
+            nc.vector.tensor_copy(x_pick[1][:], x_w[:].bitcast(U32).indirect(half_of(x_list, 1)))
+            acc = []
+            for h in range(2):
+                banks = [psum.tile([P, S], F32, name=name + "_acc%d_%d" % (h, t), tag="bank%d" % (PACK * h + t))[:, 0:HALF] for t in range(PACK)]
+                for t in range(PACK):
+                    nc.tensor.matmul_mx(
+                        out=banks[t],
+                        lhsT=d_dealt[:, t * P : (t + 1) * P].bitcast(FP8X4),
+                        lhsT_scale=placed_sc[:, t * P : (t + 1) * P],
+                        rhs=x_pick[h][:].bitcast(FP8X4),
+                        rhs_scale=picked_sc[:, S + h * HALF : S + (h + 1) * HALF],
+                        start=True,
+                        stop=True,
+                    )
+                acc.append(banks)
             return acc
 
-        b_acc = coded_product(k2_l, two_l, "b", [0, 1, 2, 3], ["slot0", "slot1", "slot2"])
+        b_acc = coded_product(k2_l, two_l, "b", ["s0", "s1", "s3", "s3", "s4", "s5"])
 
         n2_l = load_list(n2, "n2_l")
         n1_l = load_list(n1, "n1_l")
@@ -132,33 +135,30 @@ def tile_picked_twpqpullbnorm2_none_po_kernel(
         def spans(widths):
             return [slice(sum(widths[:n]), sum(widths[: n + 1])) for n in range(len(widths))]
 
-        b_val = [sb.tile([P, S], F32, name="b_val%d" % t) for t in range(PACK)]
-        b_dup = [sb.tile([P, HALF], F32, name="b_dup%d" % t) for t in range(PACK)]
-        for t in range(PACK):
-            nc.scalar.copy(b_val[t][:], b_acc[t][:])
+        b_all = sb.tile([P, PACK, S], F32, name="b_all")
+        for h in range(2):
+            for t in range(PACK):
+                nc.scalar.copy(b_all[:, t, cols(h)], b_acc[h][t])
         b_far = sb.tile([P, PACK, S], F32, name="b_far")
-        for h, rows in ((0, range(PACK)), (1, range(PACK - 2))):
-            for t in rows:
-                nc.scalar.activation(b_far[:, t, cols(h)], b_val[t][:].indirect(half_of(n2_l, h)), ACT.Copy)
+        for t in range(PACK):
+            for h in range(2):
+                nc.scalar.activation(b_far[:, t, cols(h)], b_all[:, t, :].indirect(half_of(n2_l, h)), ACT.Copy)
 
-        a_acc = coded_product(k1_l, offs_l, "a", [4, 5, 6, 7], ["slot1", "slot2", "slot3"])
-        for t in range(PACK - 2, PACK):
-            nc.sync.dma_start(b_dup[t][:], b_val[t][:, cols(1)])
+        a_acc = coded_product(k1_l, offs_l, "a", ["s4", "s1", "s6", "s5", "s0", "s7"])
         diff = sb.tile([P, PACK, S], F32, name="diff")
         for t in range(PACK):
-            if t < PACK - 2:
-                nc.vector.tensor_tensor(diff[:, t, :], b_far[:, t, :], b_val[t][:], ALU.subtract)
-            else:
-                nc.vector.tensor_tensor(diff[:, t, cols(0)], b_far[:, t, cols(0)], b_val[t][:, cols(0)], ALU.subtract)
-                nc.vector.tensor_tensor(diff[:, t, cols(1)], b_val[t][:].indirect(half_of(n2_l, 1)), b_dup[t][:], ALU.subtract)
+            engine = nc.gpsimd if t in [2, 3] else nc.vector
+            engine.tensor_tensor(diff[:, t, :], b_far[:, t, :], b_all[:, t, :], ALU.subtract)
         a_all = sb.tile([P, PACK, S], F32, name="a_all")
         th = sb.tile([P, PACK, S], F32, name="th")
         near = sb.tile([P, PACK, S], F32, name="near")
+        for h in range(2):
+            for t in range(PACK):
+                if (h, t) in []:
+                    nc.scalar.activation(a_all[:, t, cols(h)], a_acc[h][t], ACT.Copy, scale=gain[:, t : t + 1])
+                else:
+                    nc.vector.tensor_scalar(a_all[:, t, cols(h)], a_acc[h][t], gain[:, t : t + 1], None, ALU.mult)
         for t in range(PACK):
-            if t < 2:
-                nc.scalar.activation(a_all[:, t, :], a_acc[t][:], ACT.Copy, scale=gain[:, t : t + 1])
-            else:
-                nc.vector.tensor_scalar(a_all[:, t, :], a_acc[t][:], gain[:, t : t + 1], None, ALU.mult)
             nc.scalar.activation(th[:, t, :], diff[:, t, :], ACT.Tanh, scale=0.0625 * 0.5)
 
         def near_part(t, span):
@@ -169,7 +169,7 @@ def tile_picked_twpqpullbnorm2_none_po_kernel(
 
         h_val = [sb.tile([P, S], F32, name="h_val%d" % t) for t in range(PACK)]
         h_abs = [sb.tile([P, S], F32, name="h_abs%d" % t) for t in range(PACK)]
-        h_dup = [sb.tile([P, S], F32, name="h_dup%d" % t, tag="h_dup%d" % t) for t in range(PACK)]
+        h_dup = [sb.tile([P, S], F32, name="h_dup%d" % t, tag="h_dup%d" % t, align_bytes=64) for t in range(PACK)]
         order1 = [cols(0), slice(256,384), slice(384,512)]
         h_acc = []
         for n, span in enumerate(order1):
@@ -193,7 +193,7 @@ def tile_picked_twpqpullbnorm2_none_po_kernel(
             z_sc = sb.tile([P, w], U8, name="z_sc%d" % n, align_bytes=64)
             nc.vector.quantize_mx(out=z_w[:].bitcast(FP8X4), scales=z_sc[:], in_=z[:])
             if n == 0:
-                banks = [psum.tile([P, S], F32, name="h_acc0_%d" % t, tag="bank%d" % t)[:, 0:w] for t in range(PACK)]
+                banks = [psum.tile([P, S], F32, name="h_acc%d_%d" % (n, t), tag="bank%d" % t)[:, 0:w] for t in range(PACK)]
             else:
                 two_banks = [psum.tile([P, S], F32, name="h_acc%d_%d" % (n, u), tag="bank%d" % (2 + 2 * n + u)) for u in range(2)]
                 banks = [two_banks[t // 2][:, (t % 2) * w : (t % 2 + 1) * w] for t in range(PACK)]
@@ -209,8 +209,11 @@ def tile_picked_twpqpullbnorm2_none_po_kernel(
                 )
             for t in range(PACK):
                 nc.scalar.activation(h_abs[t][:, span], banks[t], ACT.Abs)
-                if n < 3:
+                if n in [0, 1, 2]:
                     nc.sync.dma_start(h_dup[t][:, span], h_abs[t][:, span])
+            if n in []:
+                for t in range(PACK):
+                    nc.scalar.copy(h_dup[t][:, span], h_abs[t][:, span])
             h_acc.append(banks)
             if n in []:
                 for t in range(PACK):
@@ -222,38 +225,40 @@ def tile_picked_twpqpullbnorm2_none_po_kernel(
                     nc.vector.tensor_copy(h_val[t][:, span], h_acc[n][t])
                 elif n not in []:
                     nc.scalar.copy(h_val[t][:, span], h_acc[n][t])
-                if n >= 3:
+                if n not in [0, 1, 2] and n not in []:
                     nc.scalar.copy(h_dup[t][:, span], h_abs[t][:, span])
 
         o_w = sb.tile([P, S], U32, name="o_w", align_bytes=64)
         o_sc = sb.tile([P, S], U8, name="o_sc", align_bytes=64)
-        order2 = [cols(0), slice(256,384), slice(384,512)]
+        order2 = [cols(0), slice(256, 448), slice(448, 512)]
         den = sb.tile([P, PACK, S], F32, name="den")
         for span in [cols(0), cols(1)]:
             for t in range(PACK):
                 nc.vector.tensor_tensor(den[:, t, span], h_abs[t][:].indirect(entries(n4_l, span)), h_dup[t][:, span], ALU.add)
         out_rows = out_0.rearrange("(p t) j -> p t j", t=PACK)
         out_words = out_1[0].rearrange("p n r -> p (n r)").bitcast(I32)
-        root = sb.tile([P, PACK, S], F32, name="root")
         inv = sb.tile([P, PACK, S], F32, name="inv")
-        for span in [cols(0), cols(1)]:
+        for h in range(2):
             for u in range(2):
                 pair = slice(2 * u, 2 * u + 2)
-                nc.scalar.activation(root[:, pair, span], den[:, pair, span], ACT.Abs_reciprocal_sqrt, bias=half_bias[:])
-                nc.scalar.activation(inv[:, pair, span], root[:, pair, span], ACT.Square)
+                root = sb.tile([P, 2, HALF], F32, name="root%d_%d" % (h, u), tag="root%d_%d" % (h, u), align_bytes=64)
+                nc.scalar.activation(root[:], den[:, pair, cols(h)], ACT.Abs_reciprocal_sqrt, bias=half_bias[:])
+                nc.scalar.activation(inv[:, pair, cols(h)], root[:], ACT.Square)
+        res_bf = [sb.tile([P, HALF * PACK], BF16, name="res_bf%d" % h, tag=["root1_0", "bf1"][h], align_bytes=64) for h in range(2)]
         for n, span in enumerate(order2):
             w = span.stop - span.start
-            res = sb.tile([P, PACK, w], F32, name="res%d" % n, tag=["h_dup2", "h_dup3", "res2"][n])
+            h = span.start // HALF
+            res = sb.tile([P, PACK, w], F32, name="res%d" % n, tag=["h_dup3", "res1", "root1_1"][n], align_bytes=64)
             for t in range(PACK):
                 nc.vector.tensor_tensor(res[:, t, :], h_val[t][:].indirect(entries(n3_l, span)), inv[:, t, span], ALU.mult)
             nc.sync.dma_start(out_rows[:, :, span], res[:])
-            res_bf = sb.tile([P, w * PACK], BF16, name="res_bf%d" % n, align_bytes=64)
             rounder = nc.scalar.copy if n < len(order2) - 1 else nc.vector.tensor_copy
             rounder(
-                res_bf[:].rearrange("p (c i t) -> p c t i", t=PACK, i=2),
+                res_bf[h][:, PACK * (span.start - h * HALF) : PACK * (span.stop - h * HALF)].rearrange("p (c i t) -> p c t i", t=PACK, i=2),
                 res[:].rearrange("p t (c i) -> p c t i", i=2),
             )
-            nc.vector.quantize_mx(out=o_w[:, span].bitcast(FP8X4), scales=o_sc[:, span], in_=res_bf[:])
-            nc.sync.dma_start(out_words[:, span], o_w[:, span].bitcast(I32))
+            if span.stop % HALF == 0:
+                nc.vector.quantize_mx(out=o_w[:, cols(h)].bitcast(FP8X4), scales=o_sc[:, cols(h)], in_=res_bf[h][:])
+                nc.sync.dma_start(out_words[:, cols(h)], o_w[:, cols(h)].bitcast(I32))
         for q in range(4):
-            (nc.sync if q < 2 else nc.scalar).dma_start(out_2[0, 4 * q : 4 * q + 4, :].bitcast(I32), o_sc[32 * q : 32 * q + 4, :].bitcast(I32))
+            (nc.sync if q < 1 else nc.scalar).dma_start(out_2[0, 4 * q : 4 * q + 4, :].bitcast(I32), o_sc[32 * q : 32 * q + 4, :].bitcast(I32))

@@ -19,8 +19,14 @@ S = 512
 T = 1024
 G = 2048
 HALF = S // 2
-LIST_COLS = S // 16
-FLOPS = 3 * 2 * 512 * 512 * 512
+QUARTER = S // 4
+ALIGN = 64
+FLOPS = 3 * 2 * S * S * S
+
+A_ON_SCALAR = 3
+B_FUSED_TILE = 3
+H_FUSED_TILES = 2
+ROUND_ON_SCALAR = 80
 
 
 def tile_picked_twpqpullbnorm2_none_po_kernel(
@@ -34,60 +40,69 @@ def tile_picked_twpqpullbnorm2_none_po_kernel(
         psum = ctx.enter_context(tc.psum_pool(name="psum", bufs=1))
 
         def load_list(src, name):
-            dst = lists.tile([P, LIST_COLS], U16, name=name)
+            dst = lists.tile([P, S // 16], U16, name=name)
             nc.sync.dma_start(dst[:], src)
             return dst
 
-        def half_of(lst, h):
-            return lst[:, h * (LIST_COLS // 2) : (h + 1) * (LIST_COLS // 2)]
-
-        def cols(h):
+        def half(h):
             return slice(h * HALF, (h + 1) * HALF)
 
-        d_sc = sb.tile([P, G], U8, name="d_sc", align_bytes=64)
-        x_sc = sb.tile([P, T], U8, name="x_sc", align_bytes=64)
+        def entries(lst, span):
+            return lst[:, span.start // 16 : span.stop // 16]
+
+        def deal(copy, dst, src, run):
+            copy(
+                dst.rearrange("p (t m i) -> p m t i", t=PACK, i=run),
+                src.rearrange("p (m i t) -> p m t i", t=PACK, i=run),
+            )
+
+        def side_by_side(packed):
+            return packed.rearrange("p (c i t) -> p c t i", t=PACK, i=2)
+
+        def by_pairs(rows):
+            return rows.rearrange("p t (c i) -> p c t i", i=2)
+
+        def load_scale_rows(dst, src):
+            for q in range(4):
+                nc.sync.dma_start(dst[32 * q : 32 * q + 4, :].bitcast(I32), src[4 * q : 4 * q + 4, :].bitcast(I32))
+
+        d_sc = sb.tile([P, G], U8, name="d_sc", align_bytes=ALIGN)
+        x_sc = sb.tile([P, T], U8, name="x_sc", align_bytes=ALIGN)
         nc.gpsimd.memset(d_sc[:].bitcast(I32), 0)
         nc.vector.memset(x_sc[:].bitcast(I32), 0)
         k2_l = load_list(k2, "k2_l")
         nc.sync.dma_start(d_sc[0:P:8, :].bitcast(I32), d_scales[0].bitcast(I32))
         two_l = load_list(two, "two_l")
-        for q in range(4):
-            nc.sync.dma_start(x_sc[32 * q : 32 * q + 4, :].bitcast(I32), x_scales[0, 4 * q : 4 * q + 4, :].bitcast(I32))
-        x_w = sb.tile([P, T], I32, name="x_w", align_bytes=64)
-        d_w = sb.tile([P, G], I32, name="d_w", align_bytes=64)
-        nc.sync.dma_start(x_w[:], x_words[0].rearrange("p n r -> p (n r)").bitcast(I32))
+        x_w = sb.tile([P, T], I32, name="x_w", align_bytes=ALIGN)
+        d_w = sb.tile([P, G], I32, name="d_w", align_bytes=ALIGN)
         nc.sync.dma_start(d_w[:], d_words[0].rearrange("p n r -> p (n r)").bitcast(I32))
-        k1_l = load_list(k1, "k1_l")
-        offs_l = load_list(offs, "offs_l")
-        gain_raw = sb.tile([P, PACK], F32, name="gain_raw")
-        nc.gpsimd.dma_start(gain_raw[:], gn.rearrange("(p t) o -> p (t o)", t=PACK))
-
+        load_scale_rows(x_sc, x_scales[0])
+        nc.sync.dma_start(x_w[:], x_words[0].rearrange("p n r -> p (n r)").bitcast(I32))
+        gn_rows = sb.tile([P, PACK], F32, name="gn_rows")
+        nc.gpsimd.dma_start(gn_rows[:], gn.rearrange("(p t) o -> p (t o)", t=PACK))
         gain = sb.tile([P, PACK], F32, name="gain")
-        nc.scalar.activation(gain[:], gain_raw[:], ACT.Copy, scale=0.0625 * 0.5)
+        nc.scalar.activation(gain[:], gn_rows[:], ACT.Copy, scale=0.0625 * 0.5)
 
         def coded_product(d_list, x_list, name, slots):
-            picked_sc = sb.tile([P, 2 * S], U8, name=name + "_picked_sc", tag=slots[0], align_bytes=64)
+            picked_sc = sb.tile([P, 2 * S], U8, name=name + "_picked_sc", tag=slots["sc"], align_bytes=ALIGN)
             nc.vector.tensor_copy(picked_sc[:, 0:S], d_sc[:].indirect(d_list[:]))
             nc.vector.tensor_copy(picked_sc[:, S : 2 * S], x_sc[:].indirect(x_list[:]))
-            placed_sc = sb.tile([P, S], U8, name=name + "_placed_sc", align_bytes=64)
-            nc.vector.tensor_copy(
-                placed_sc[:, 0:S].rearrange("p (t m i) -> p m t i", t=PACK, i=16),
-                picked_sc[:, 0:S].rearrange("p (m i t) -> p m t i", t=PACK, i=16),
-            )
+            dealt_sc = sb.tile([P, S], U8, name=name + "_dealt_sc", align_bytes=ALIGN)
+            deal(nc.vector.tensor_copy, dealt_sc[:], picked_sc[:, 0:S], 16)
             for c in range(1, 4):
-                nc.sync.dma_start(placed_sc[c:P:32, :].bitcast(I32), placed_sc[8 * c : P : 32, :].bitcast(I32))
-            d_pick = [sb.tile([P, HALF], U32, name=name + "_d_pick%d" % h, tag=slots[3 + h], align_bytes=64) for h in range(2)]
-            x_pick = [sb.tile([P, HALF], U32, name=name + "_x_pick%d" % h, tag=slots[1 + h], align_bytes=64) for h in range(2)]
-            d_dealt = sb.tile([P, S], U32, name=name + "_d_dealt", tag=slots[5], align_bytes=64)
-            nc.vector.tensor_copy(x_pick[0][:], x_w[:].bitcast(U32).indirect(half_of(x_list, 0)))
+                nc.sync.dma_start(dealt_sc[c:P:32, :].bitcast(I32), dealt_sc[8 * c : P : 32, :].bitcast(I32))
+            d_pick = [sb.tile([P, HALF], U32, name=name + "_d_pick%d" % h, tag=slots["d"][h], align_bytes=ALIGN) for h in range(2)]
+            x_pick = [sb.tile([P, HALF], U32, name=name + "_x_pick%d" % h, tag="x_pick%d" % h, align_bytes=ALIGN) for h in range(2)]
+            d_dealt = sb.tile([P, S], U32, name=name + "_d_dealt", tag=slots["dealt"], align_bytes=ALIGN)
             for h in range(2):
-                nc.vector.tensor_copy(d_pick[h][:], d_w[:].bitcast(U32).indirect(half_of(d_list, h)))
+                nc.vector.tensor_copy(d_pick[h][:], d_w[:].bitcast(U32).indirect(entries(d_list, half(h))))
             for h in range(2):
                 nc.vector.tensor_copy(
                     d_dealt[:].rearrange("p (t h m i) -> p h m t i", t=PACK, h=2, i=4)[:, h],
                     d_pick[h][:].rearrange("p (m i t) -> p m t i", t=PACK, i=4),
                 )
-            nc.vector.tensor_copy(x_pick[1][:], x_w[:].bitcast(U32).indirect(half_of(x_list, 1)))
+            for h in range(2):
+                nc.vector.tensor_copy(x_pick[h][:], x_w[:].bitcast(U32).indirect(entries(x_list, half(h))))
             acc = []
             for h in range(2):
                 banks = [psum.tile([P, S], F32, name=name + "_acc%d_%d" % (h, t), tag="bank%d" % (PACK * h + t))[:, 0:HALF] for t in range(PACK)]
@@ -95,7 +110,7 @@ def tile_picked_twpqpullbnorm2_none_po_kernel(
                     nc.tensor.matmul_mx(
                         out=banks[t],
                         lhsT=d_dealt[:, t * P : (t + 1) * P].bitcast(FP8X4),
-                        lhsT_scale=placed_sc[:, t * P : (t + 1) * P],
+                        lhsT_scale=dealt_sc[:, t * P : (t + 1) * P],
                         rhs=x_pick[h][:].bitcast(FP8X4),
                         rhs_scale=picked_sc[:, S + h * HALF : S + (h + 1) * HALF],
                         start=True,
@@ -104,99 +119,86 @@ def tile_picked_twpqpullbnorm2_none_po_kernel(
                 acc.append(banks)
             return acc
 
-        b_acc = coded_product(k2_l, two_l, "b", ["s0", "s1", "s3", "s3", "s4", "s5"])
+        b_acc = coded_product(k2_l, two_l, "b", {"sc": "slot0", "d": ["slot1", "slot2"], "dealt": "slot3"})
 
+        k1_l = load_list(k1, "k1_l")
+        offs_l = load_list(offs, "offs_l")
         n2_l = load_list(n2, "n2_l")
         n1_l = load_list(n1, "n1_l")
         n4_l = load_list(n4, "n4_l")
         n3_l = load_list(n3, "n3_l")
-        w_raw = sb.tile([P, 2 * S], U8, name="w_raw", align_bytes=64)
+        w_raw = sb.tile([P, 2 * S], U8, name="w_raw", align_bytes=ALIGN)
         nc.gpsimd.dma_start(w_raw[:].bitcast(I32), w1_words[0].bitcast(I32))
-        w_sc_raw = sb.tile([P, S], U8, name="w_sc_raw", align_bytes=64)
-        nc.gpsimd.memset(w_sc_raw[:].bitcast(I32), 0)
-        for q in range(4):
-            nc.gpsimd.dma_start(w_sc_raw[32 * q : 32 * q + 4, :].bitcast(I32), w1_scales[0, 4 * q : 4 * q + 4, :].bitcast(I32))
-        w_dealt = sb.tile([P, 2 * S], U8, name="w_dealt", align_bytes=64)
-        nc.scalar.copy(
-            w_dealt[:].bitcast(U16).rearrange("p (t m i) -> p m t i", t=PACK, i=8),
-            w_raw[:].bitcast(U16).rearrange("p (m i t) -> p m t i", t=PACK, i=8),
-        )
-        w_sc = sb.tile([P, S], U8, name="w_sc", align_bytes=64)
-        nc.gpsimd.tensor_copy(
-            w_sc[:].rearrange("p (t m i) -> p m t i", t=PACK, i=16),
-            w_sc_raw[:].rearrange("p (m i t) -> p m t i", t=PACK, i=16),
-        )
-        half_bias = sb.tile([P, 1], F32, name="half_bias")
-        nc.gpsimd.memset(half_bias[:], 0.5)
+        w_dealt = sb.tile([P, 2 * S], U8, name="w_dealt", align_bytes=ALIGN)
+        deal(nc.scalar.copy, w_dealt[:].bitcast(U16), w_raw[:].bitcast(U16), 8)
+        one_half = sb.tile([P, 1], F32, name="one_half")
+        nc.gpsimd.memset(one_half[:], 0.5)
 
-        def entries(lst, span):
-            return lst[:, span.start // 16 : span.stop // 16]
-
-        def spans(widths):
-            return [slice(sum(widths[:n]), sum(widths[: n + 1])) for n in range(len(widths))]
-
-        b_all = sb.tile([P, PACK, S], F32, name="b_all")
+        b_val = [sb.tile([P, S], F32, name="b_val%d" % t) for t in range(PACK)]
         for h in range(2):
             for t in range(PACK):
-                nc.scalar.copy(b_all[:, t, cols(h)], b_acc[h][t])
+                nc.scalar.copy(b_val[t][:, half(h)], b_acc[h][t])
         b_far = sb.tile([P, PACK, S], F32, name="b_far")
         for t in range(PACK):
-            for h in range(2):
-                nc.scalar.activation(b_far[:, t, cols(h)], b_all[:, t, :].indirect(half_of(n2_l, h)), ACT.Copy)
+            for h in range(1 if t == B_FUSED_TILE else 2):
+                nc.scalar.activation(b_far[:, t, half(h)], b_val[t][:].indirect(entries(n2_l, half(h))), ACT.Copy)
 
-        a_acc = coded_product(k1_l, offs_l, "a", ["s4", "s1", "s6", "s5", "s0", "s7"])
+        a_acc = coded_product(k1_l, offs_l, "a", {"sc": "slot2", "d": ["slot3", "slot0"], "dealt": "slot4"})
+
+        b_copy = sb.tile([P, HALF], F32, name="b_copy")
+        nc.sync.dma_start(b_copy[:], b_val[B_FUSED_TILE][:, half(1)])
+        w_sc_raw = sb.tile([P, S], U8, name="w_sc_raw", align_bytes=ALIGN)
+        nc.gpsimd.memset(w_sc_raw[:].bitcast(I32), 0)
+        load_scale_rows(w_sc_raw, w1_scales[0])
+
         diff = sb.tile([P, PACK, S], F32, name="diff")
         for t in range(PACK):
-            engine = nc.gpsimd if t in [2, 3] else nc.vector
-            engine.tensor_tensor(diff[:, t, :], b_far[:, t, :], b_all[:, t, :], ALU.subtract)
-        a_all = sb.tile([P, PACK, S], F32, name="a_all")
+            if t == B_FUSED_TILE:
+                nc.vector.tensor_tensor(diff[:, t, half(0)], b_far[:, t, half(0)], b_val[t][:, half(0)], ALU.subtract)
+                nc.vector.tensor_tensor(diff[:, t, half(1)], b_val[t][:].indirect(entries(n2_l, half(1))), b_copy[:], ALU.subtract)
+            else:
+                nc.vector.tensor_tensor(diff[:, t, :], b_far[:, t, :], b_val[t][:], ALU.subtract)
+        a_half = sb.tile([P, PACK, S], F32, name="a_half")
         th = sb.tile([P, PACK, S], F32, name="th")
         near = sb.tile([P, PACK, S], F32, name="near")
         for h in range(2):
             for t in range(PACK):
-                if (h, t) in []:
-                    nc.scalar.activation(a_all[:, t, cols(h)], a_acc[h][t], ACT.Copy, scale=gain[:, t : t + 1])
+                if PACK * h + t < A_ON_SCALAR:
+                    nc.scalar.activation(a_half[:, t, half(h)], a_acc[h][t], ACT.Copy, scale=gain[:, t : t + 1])
                 else:
-                    nc.vector.tensor_scalar(a_all[:, t, cols(h)], a_acc[h][t], gain[:, t : t + 1], None, ALU.mult)
+                    nc.vector.tensor_scalar(a_half[:, t, half(h)], a_acc[h][t], gain[:, t : t + 1], None, ALU.mult)
         for t in range(PACK):
             nc.scalar.activation(th[:, t, :], diff[:, t, :], ACT.Tanh, scale=0.0625 * 0.5)
-
-        def near_part(t, span):
-            nc.vector.scalar_tensor_tensor(near[:, t, span], th[:, t, span], 1.0, a_all[:, t, span], ALU.subtract, ALU.mult)
-
         for t in range(PACK):
-            near_part(t, slice(0, S))
+            nc.vector.scalar_tensor_tensor(near[:, t, :], th[:, t, :], 1.0, a_half[:, t, :], ALU.subtract, ALU.mult)
+        w_sc = sb.tile([P, S], U8, name="w_sc", align_bytes=ALIGN)
+        deal(nc.vector.tensor_copy, w_sc[:], w_sc_raw[:], 16)
 
+        stretches = [half(0), slice(HALF, HALF + QUARTER), slice(HALF + QUARTER, S)]
         h_val = [sb.tile([P, S], F32, name="h_val%d" % t) for t in range(PACK)]
-        h_abs = [sb.tile([P, S], F32, name="h_abs%d" % t) for t in range(PACK)]
-        h_dup = [sb.tile([P, S], F32, name="h_dup%d" % t, tag="h_dup%d" % t, align_bytes=64) for t in range(PACK)]
-        order1 = [cols(0), slice(256,384), slice(384,512)]
+        h_abs = [sb.tile([P, S], F32, name="h_abs%d" % t, tag="h_abs%d" % t, align_bytes=ALIGN) for t in range(PACK)]
+        abs_copy = [sb.tile([P, S], F32, name="abs_copy%d" % t) for t in range(PACK)]
         h_acc = []
-        for n, span in enumerate(order1):
-            w = span.stop - span.start
-            a_far = sb.tile([P, PACK, w], F32, name="a_far%d" % n, tag="a_far%d" % n)
+        for n, span in enumerate(stretches):
+            width = span.stop - span.start
+            a_far = sb.tile([P, PACK, width], F32, name="a_far%d" % n, tag="a_far%d" % n)
             for t in range(PACK):
-                nc.scalar.activation(a_far[:, t, :], a_all[:, t, :].indirect(entries(n1_l, span)), ACT.Copy)
-            far = sb.tile([P, PACK, w], F32, name="far%d" % n, tag="a_far%d" % (n - 1))
-            for u in range(2 if n == 0 else 1):
-                k = PACK // (2 if n == 0 else 1)
-                rows = slice(u * k, (u + 1) * k)
+                nc.scalar.activation(a_far[:, t, :], a_half[:, t, :].indirect(entries(n1_l, span)), ACT.Copy)
+            far = sb.tile([P, PACK, width], F32, name="far%d" % n, tag="a_far%d" % (n - 1))
+            step = PACK * QUARTER // width
+            for t in range(0, PACK, step):
+                rows = slice(t, t + step)
                 nc.vector.scalar_tensor_tensor(far[:, rows, :], th[:, rows, span], 1.0, a_far[:, rows, :], ALU.add, ALU.mult)
-            z = sb.tile([P, w * PACK], BF16, name="z%d" % n, align_bytes=64)
-            nc.vector.tensor_tensor(
-                z[:].rearrange("p (c i t) -> p c t i", t=PACK, i=2),
-                far[:].rearrange("p t (c i) -> p c t i", i=2),
-                near[:, :, span].rearrange("p t (c i) -> p c t i", i=2),
-                ALU.subtract,
-            )
-            z_w = sb.tile([P, w], U32, name="z_w%d" % n, align_bytes=64)
-            z_sc = sb.tile([P, w], U8, name="z_sc%d" % n, align_bytes=64)
+            z = sb.tile([P, width * PACK], BF16, name="z%d" % n, align_bytes=ALIGN)
+            nc.vector.tensor_tensor(side_by_side(z[:]), by_pairs(far[:]), by_pairs(near[:, :, span]), ALU.subtract)
+            z_w = sb.tile([P, width], U32, name="z_w%d" % n, align_bytes=ALIGN)
+            z_sc = sb.tile([P, width], U8, name="z_sc%d" % n, align_bytes=ALIGN)
             nc.vector.quantize_mx(out=z_w[:].bitcast(FP8X4), scales=z_sc[:], in_=z[:])
-            if n == 0:
-                banks = [psum.tile([P, S], F32, name="h_acc%d_%d" % (n, t), tag="bank%d" % t)[:, 0:w] for t in range(PACK)]
+            if width == HALF:
+                banks = [psum.tile([P, S], F32, name="h_acc%d_%d" % (n, t), tag="bank%d" % t)[:, 0:width] for t in range(PACK)]
             else:
-                two_banks = [psum.tile([P, S], F32, name="h_acc%d_%d" % (n, u), tag="bank%d" % (2 + 2 * n + u)) for u in range(2)]
-                banks = [two_banks[t // 2][:, (t % 2) * w : (t % 2 + 1) * w] for t in range(PACK)]
+                shared = [psum.tile([P, S], F32, name="h_acc%d_%d" % (n, u), tag="bank%d" % (2 + 2 * n + u)) for u in range(2)]
+                banks = [shared[t // 2][:, (t % 2) * width : (t % 2 + 1) * width] for t in range(PACK)]
             for t in range(PACK):
                 nc.tensor.matmul_mx(
                     out=banks[t],
@@ -207,58 +209,53 @@ def tile_picked_twpqpullbnorm2_none_po_kernel(
                     start=True,
                     stop=True,
                 )
+            done = half(span.start // HALF)
             for t in range(PACK):
                 nc.scalar.activation(h_abs[t][:, span], banks[t], ACT.Abs)
-                if n in [0, 1, 2]:
-                    nc.sync.dma_start(h_dup[t][:, span], h_abs[t][:, span])
-            if n in []:
-                for t in range(PACK):
-                    nc.scalar.copy(h_dup[t][:, span], h_abs[t][:, span])
+                if span.stop == done.stop and (n, t) != (0, 0):
+                    nc.sync.dma_start(abs_copy[t][:, done], h_abs[t][:, done])
+            if n == 0:
+                nc.scalar.copy(abs_copy[0][:, done], h_abs[0][:, done])
             h_acc.append(banks)
-            if n in []:
-                for t in range(PACK):
-                    nc.scalar.copy(h_val[t][:, span], banks[t])
-        for n, span in enumerate(order1):
-            w = span.stop - span.start
+        for n, span in enumerate(stretches):
+            copy = nc.scalar.copy if span.stop == S else nc.vector.tensor_copy
             for t in range(PACK):
-                if n in [0, 1]:
-                    nc.vector.tensor_copy(h_val[t][:, span], h_acc[n][t])
-                elif n not in []:
-                    nc.scalar.copy(h_val[t][:, span], h_acc[n][t])
-                if n not in [0, 1, 2] and n not in []:
-                    nc.scalar.copy(h_dup[t][:, span], h_abs[t][:, span])
+                copy(h_val[t][:, span], h_acc[n][t])
 
-        o_w = sb.tile([P, S], U32, name="o_w", align_bytes=64)
-        o_sc = sb.tile([P, S], U8, name="o_sc", align_bytes=64)
-        order2 = [cols(0), slice(256, 448), slice(448, 512)]
+        h_far = sb.tile([P, PACK - H_FUSED_TILES, HALF], F32, name="h_far")
+        for t in range(H_FUSED_TILES, PACK):
+            nc.scalar.activation(h_far[:, t - H_FUSED_TILES, :], h_val[t][:].indirect(entries(n3_l, half(1))), ACT.Copy)
         den = sb.tile([P, PACK, S], F32, name="den")
-        for span in [cols(0), cols(1)]:
+        for h in range(2):
             for t in range(PACK):
-                nc.vector.tensor_tensor(den[:, t, span], h_abs[t][:].indirect(entries(n4_l, span)), h_dup[t][:, span], ALU.add)
-        out_rows = out_0.rearrange("(p t) j -> p t j", t=PACK)
-        out_words = out_1[0].rearrange("p n r -> p (n r)").bitcast(I32)
+                nc.vector.tensor_tensor(den[:, t, half(h)], h_abs[t][:].indirect(entries(n4_l, half(h))), abs_copy[t][:, half(h)], ALU.add)
         inv = sb.tile([P, PACK, S], F32, name="inv")
         for h in range(2):
-            for u in range(2):
-                pair = slice(2 * u, 2 * u + 2)
-                root = sb.tile([P, 2, HALF], F32, name="root%d_%d" % (h, u), tag="root%d_%d" % (h, u), align_bytes=64)
-                nc.scalar.activation(root[:], den[:, pair, cols(h)], ACT.Abs_reciprocal_sqrt, bias=half_bias[:])
-                nc.scalar.activation(inv[:, pair, cols(h)], root[:], ACT.Square)
-        res_bf = [sb.tile([P, HALF * PACK], BF16, name="res_bf%d" % h, tag=["root1_0", "bf1"][h], align_bytes=64) for h in range(2)]
-        for n, span in enumerate(order2):
-            w = span.stop - span.start
-            h = span.start // HALF
-            res = sb.tile([P, PACK, w], F32, name="res%d" % n, tag=["h_dup3", "res1", "root1_1"][n], align_bytes=64)
             for t in range(PACK):
-                nc.vector.tensor_tensor(res[:, t, :], h_val[t][:].indirect(entries(n3_l, span)), inv[:, t, span], ALU.mult)
-            nc.sync.dma_start(out_rows[:, :, span], res[:])
-            rounder = nc.scalar.copy if n < len(order2) - 1 else nc.vector.tensor_copy
-            rounder(
-                res_bf[h][:, PACK * (span.start - h * HALF) : PACK * (span.stop - h * HALF)].rearrange("p (c i t) -> p c t i", t=PACK, i=2),
-                res[:].rearrange("p t (c i) -> p c t i", i=2),
-            )
-            if span.stop % HALF == 0:
-                nc.vector.quantize_mx(out=o_w[:, cols(h)].bitcast(FP8X4), scales=o_sc[:, cols(h)], in_=res_bf[h][:])
-                nc.sync.dma_start(out_words[:, cols(h)], o_w[:, cols(h)].bitcast(I32))
+                root = sb.tile([P, HALF], F32, name="root%d_%d" % (h, t), tag="root%d_%d" % (h, t), align_bytes=ALIGN)
+                nc.scalar.activation(root[:], den[:, t, half(h)], ACT.Abs_reciprocal_sqrt, bias=one_half[:])
+                nc.scalar.activation(inv[:, t, half(h)], root[:], ACT.Square)
+
+        out_rows = out_0.rearrange("(p t) j -> p t j", t=PACK)
+        out_words = out_1[0].rearrange("p n r -> p (n r)").bitcast(I32)
+        o_w = sb.tile([P, S], U32, name="o_w", align_bytes=ALIGN)
+        o_sc = sb.tile([P, S], U8, name="o_sc", align_bytes=ALIGN)
+        res = [sb.tile([P, PACK, HALF], F32, name="res%d" % h, tag=("h_abs3", "res1")[h], align_bytes=ALIGN) for h in range(2)]
+        res_bf = [sb.tile([P, HALF * PACK], BF16, name="res_bf%d" % h, tag=("root1_2", "res_bf1")[h], align_bytes=ALIGN) for h in range(2)]
+        for h in range(2):
+            fused = PACK if h == 0 else H_FUSED_TILES
+            for t in range(fused):
+                nc.vector.tensor_tensor(res[h][:, t, :], h_val[t][:].indirect(entries(n3_l, half(h))), inv[:, t, half(h)], ALU.mult)
+            if fused < PACK:
+                nc.vector.tensor_tensor(res[h][:, fused:PACK, :], h_far[:], inv[:, fused:PACK, half(h)], ALU.mult)
+            for t in range(0, PACK, 2):
+                nc.sync.dma_start(out_rows[:, t : t + 2, half(h)], res[h][:, t : t + 2, :])
+            cut = HALF if h == 0 else ROUND_ON_SCALAR
+            nc.scalar.copy(side_by_side(res_bf[h][:, 0 : PACK * cut]), by_pairs(res[h][:, :, 0:cut]))
+            if cut < HALF:
+                nc.vector.tensor_copy(side_by_side(res_bf[h][:, PACK * cut :]), by_pairs(res[h][:, :, cut:]))
+            nc.vector.quantize_mx(out=o_w[:, half(h)].bitcast(FP8X4), scales=o_sc[:, half(h)], in_=res_bf[h][:])
+            nc.sync.dma_start(out_words[:, half(h)], o_w[:, half(h)].bitcast(I32))
         for q in range(4):
-            (nc.sync if q < 1 else nc.scalar).dma_start(out_2[0, 4 * q : 4 * q + 4, :].bitcast(I32), o_sc[32 * q : 32 * q + 4, :].bitcast(I32))
+            queue = nc.sync if q == 0 else nc.scalar
+            queue.dma_start(out_2[0, 4 * q : 4 * q + 4, :].bitcast(I32), o_sc[32 * q : 32 * q + 4, :].bitcast(I32))

from contextlib import ExitStack

import concourse.mybir as mybir

F32 = mybir.dt.float32
BF16 = mybir.dt.bfloat16
I32 = mybir.dt.int32
U32 = mybir.dt.uint32
U16 = mybir.dt.uint16
U8 = mybir.dt.uint8
FP8X4 = mybir.dt.float8_e4m3fn_x4
FP4X4 = mybir.dt.float4_e2m1fn_x4
ACT = mybir.ActivationFunctionType
ALU = mybir.AluOpType

P = 128
PACK = 4
S = 512
T = 1024
G = 2048
HALF = S // 2
QUARTER = S // 4
ALIGN = 64
FLOPS = 3 * 2 * S * S * S

A_ON_SCALAR = 3
B_FUSED_TILE = 3
H_FUSED_TILES = 2
ROUND_ON_SCALAR = 80


def tile_picked_twpqpullbnorm2_none_po_kernel(
    tc, x_words, x_scales, d_words, d_scales, gn, w1_words, w1_scales,
    offs, k1, two, k2, n1, n2, n3, n4, out_0, out_1, out_2,
):
    nc = tc.nc
    with ExitStack() as ctx:
        lists = ctx.enter_context(tc.tile_pool(name="lists", bufs=1))
        sb = ctx.enter_context(tc.tile_pool(name="sb", bufs=1))
        psum = ctx.enter_context(tc.psum_pool(name="psum", bufs=1))

        def load_list(src, name):
            dst = lists.tile([P, S // 16], U16, name=name)
            nc.sync.dma_start(dst[:], src)
            return dst

        def half(h):
            return slice(h * HALF, (h + 1) * HALF)

        def entries(lst, span):
            return lst[:, span.start // 16 : span.stop // 16]

        def deal(copy, dst, src, run):
            copy(
                dst.rearrange("p (t m i) -> p m t i", t=PACK, i=run),
                src.rearrange("p (m i t) -> p m t i", t=PACK, i=run),
            )

        def side_by_side(packed):
            return packed.rearrange("p (c i t) -> p c t i", t=PACK, i=2)

        def by_pairs(rows):
            return rows.rearrange("p t (c i) -> p c t i", i=2)

        def load_scale_rows(dst, src):
            for q in range(4):
                nc.sync.dma_start(dst[32 * q : 32 * q + 4, :].bitcast(I32), src[4 * q : 4 * q + 4, :].bitcast(I32))

        d_sc = sb.tile([P, G], U8, name="d_sc", align_bytes=ALIGN)
        x_sc = sb.tile([P, T], U8, name="x_sc", align_bytes=ALIGN)
        nc.gpsimd.memset(d_sc[:].bitcast(I32), 0)
        nc.vector.memset(x_sc[:].bitcast(I32), 0)
        k2_l = load_list(k2, "k2_l")
        nc.sync.dma_start(d_sc[0:P:8, :].bitcast(I32), d_scales[0].bitcast(I32))
        two_l = load_list(two, "two_l")
        x_w = sb.tile([P, T], I32, name="x_w", align_bytes=ALIGN)
        d_w = sb.tile([P, G], I32, name="d_w", align_bytes=ALIGN)
        nc.sync.dma_start(d_w[:], d_words[0].rearrange("p n r -> p (n r)").bitcast(I32))
        load_scale_rows(x_sc, x_scales[0])
        nc.sync.dma_start(x_w[:], x_words[0].rearrange("p n r -> p (n r)").bitcast(I32))
        gn_rows = sb.tile([P, PACK], F32, name="gn_rows")
        nc.gpsimd.dma_start(gn_rows[:], gn.rearrange("(p t) o -> p (t o)", t=PACK))
        gain = sb.tile([P, PACK], F32, name="gain")
        nc.scalar.activation(gain[:], gn_rows[:], ACT.Copy, scale=0.0625 * 0.5)

        def coded_product(d_list, x_list, name, slots):
            picked_sc = sb.tile([P, 2 * S], U8, name=name + "_picked_sc", tag=slots["sc"], align_bytes=ALIGN)
            nc.vector.tensor_copy(picked_sc[:, 0:S], d_sc[:].indirect(d_list[:]))
            nc.vector.tensor_copy(picked_sc[:, S : 2 * S], x_sc[:].indirect(x_list[:]))
            dealt_sc = sb.tile([P, S], U8, name=name + "_dealt_sc", align_bytes=ALIGN)
            deal(nc.vector.tensor_copy, dealt_sc[:], picked_sc[:, 0:S], 16)
            for c in range(1, 4):
                nc.sync.dma_start(dealt_sc[c:P:32, :].bitcast(I32), dealt_sc[8 * c : P : 32, :].bitcast(I32))
            d_pick = [sb.tile([P, HALF], U32, name=name + "_d_pick%d" % h, tag=slots["d"][h], align_bytes=ALIGN) for h in range(2)]
            x_pick = [sb.tile([P, HALF], U32, name=name + "_x_pick%d" % h, tag="x_pick%d" % h, align_bytes=ALIGN) for h in range(2)]
            d_dealt = sb.tile([P, S], U32, name=name + "_d_dealt", tag=slots["dealt"], align_bytes=ALIGN)
            for h in range(2):
                nc.vector.tensor_copy(d_pick[h][:], d_w[:].bitcast(U32).indirect(entries(d_list, half(h))))
            for h in range(2):
                nc.vector.tensor_copy(
                    d_dealt[:].rearrange("p (t h m i) -> p h m t i", t=PACK, h=2, i=4)[:, h],
                    d_pick[h][:].rearrange("p (m i t) -> p m t i", t=PACK, i=4),
                )
            for h in range(2):
                nc.vector.tensor_copy(x_pick[h][:], x_w[:].bitcast(U32).indirect(entries(x_list, half(h))))
            acc = []
            for h in range(2):
                banks = [psum.tile([P, S], F32, name=name + "_acc%d_%d" % (h, t), tag="bank%d" % (PACK * h + t))[:, 0:HALF] for t in range(PACK)]
                for t in range(PACK):
                    nc.tensor.matmul_mx(
                        out=banks[t],
                        lhsT=d_dealt[:, t * P : (t + 1) * P].bitcast(FP8X4),
                        lhsT_scale=dealt_sc[:, t * P : (t + 1) * P],
                        rhs=x_pick[h][:].bitcast(FP8X4),
                        rhs_scale=picked_sc[:, S + h * HALF : S + (h + 1) * HALF],
                        start=True,
                        stop=True,
                    )
                acc.append(banks)
            return acc

        b_acc = coded_product(k2_l, two_l, "b", {"sc": "slot0", "d": ["slot1", "slot2"], "dealt": "slot3"})

        k1_l = load_list(k1, "k1_l")
        offs_l = load_list(offs, "offs_l")
        n2_l = load_list(n2, "n2_l")
        n1_l = load_list(n1, "n1_l")
        n4_l = load_list(n4, "n4_l")
        n3_l = load_list(n3, "n3_l")
        w_raw = sb.tile([P, 2 * S], U8, name="w_raw", align_bytes=ALIGN)
        nc.gpsimd.dma_start(w_raw[:].bitcast(I32), w1_words[0].bitcast(I32))
        w_dealt = sb.tile([P, 2 * S], U8, name="w_dealt", align_bytes=ALIGN)
        deal(nc.scalar.copy, w_dealt[:].bitcast(U16), w_raw[:].bitcast(U16), 8)
        one_half = sb.tile([P, 1], F32, name="one_half")
        nc.gpsimd.memset(one_half[:], 0.5)

        b_val = [sb.tile([P, S], F32, name="b_val%d" % t) for t in range(PACK)]
        for h in range(2):
            for t in range(PACK):
                nc.scalar.copy(b_val[t][:, half(h)], b_acc[h][t])
        b_far = sb.tile([P, PACK, S], F32, name="b_far")
        for t in range(PACK):
            for h in range(1 if t == B_FUSED_TILE else 2):
                nc.scalar.activation(b_far[:, t, half(h)], b_val[t][:].indirect(entries(n2_l, half(h))), ACT.Copy)

        a_acc = coded_product(k1_l, offs_l, "a", {"sc": "slot2", "d": ["slot3", "slot0"], "dealt": "slot4"})

        b_copy = sb.tile([P, HALF], F32, name="b_copy")
        nc.sync.dma_start(b_copy[:], b_val[B_FUSED_TILE][:, half(1)])
        w_sc_raw = sb.tile([P, S], U8, name="w_sc_raw", align_bytes=ALIGN)
        nc.gpsimd.memset(w_sc_raw[:].bitcast(I32), 0)
        load_scale_rows(w_sc_raw, w1_scales[0])

        diff = sb.tile([P, PACK, S], F32, name="diff")
        for t in range(PACK):
            if t == B_FUSED_TILE:
                nc.vector.tensor_tensor(diff[:, t, half(0)], b_far[:, t, half(0)], b_val[t][:, half(0)], ALU.subtract)
                nc.vector.tensor_tensor(diff[:, t, half(1)], b_val[t][:].indirect(entries(n2_l, half(1))), b_copy[:], ALU.subtract)
            else:
                nc.vector.tensor_tensor(diff[:, t, :], b_far[:, t, :], b_val[t][:], ALU.subtract)
        a_half = sb.tile([P, PACK, S], F32, name="a_half")
        th = sb.tile([P, PACK, S], F32, name="th")
        near = sb.tile([P, PACK, S], F32, name="near")
        for h in range(2):
            for t in range(PACK):
                if PACK * h + t < A_ON_SCALAR:
                    nc.scalar.activation(a_half[:, t, half(h)], a_acc[h][t], ACT.Copy, scale=gain[:, t : t + 1])
                else:
                    nc.vector.tensor_scalar(a_half[:, t, half(h)], a_acc[h][t], gain[:, t : t + 1], None, ALU.mult)
        for t in range(PACK):
            nc.scalar.activation(th[:, t, :], diff[:, t, :], ACT.Tanh, scale=0.0625 * 0.5)
        for t in range(PACK):
            nc.vector.scalar_tensor_tensor(near[:, t, :], th[:, t, :], 1.0, a_half[:, t, :], ALU.subtract, ALU.mult)
        w_sc = sb.tile([P, S], U8, name="w_sc", align_bytes=ALIGN)
        deal(nc.vector.tensor_copy, w_sc[:], w_sc_raw[:], 16)

        stretches = [half(0), slice(HALF, HALF + QUARTER), slice(HALF + QUARTER, S)]
        h_val = [sb.tile([P, S], F32, name="h_val%d" % t) for t in range(PACK)]
        h_abs = [sb.tile([P, S], F32, name="h_abs%d" % t, tag="h_abs%d" % t, align_bytes=ALIGN) for t in range(PACK)]
        abs_copy = [sb.tile([P, S], F32, name="abs_copy%d" % t) for t in range(PACK)]
        h_acc = []
        for n, span in enumerate(stretches):
            width = span.stop - span.start
            a_far = sb.tile([P, PACK, width], F32, name="a_far%d" % n, tag="a_far%d" % n)
            for t in range(PACK):
                nc.scalar.activation(a_far[:, t, :], a_half[:, t, :].indirect(entries(n1_l, span)), ACT.Copy)
            far = sb.tile([P, PACK, width], F32, name="far%d" % n, tag="a_far%d" % (n - 1))
            step = PACK * QUARTER // width
            for t in range(0, PACK, step):
                rows = slice(t, t + step)
                nc.vector.scalar_tensor_tensor(far[:, rows, :], th[:, rows, span], 1.0, a_far[:, rows, :], ALU.add, ALU.mult)
            z = sb.tile([P, width * PACK], BF16, name="z%d" % n, align_bytes=ALIGN)
            nc.vector.tensor_tensor(side_by_side(z[:]), by_pairs(far[:]), by_pairs(near[:, :, span]), ALU.subtract)
            z_w = sb.tile([P, width], U32, name="z_w%d" % n, align_bytes=ALIGN)
            z_sc = sb.tile([P, width], U8, name="z_sc%d" % n, align_bytes=ALIGN)
            nc.vector.quantize_mx(out=z_w[:].bitcast(FP8X4), scales=z_sc[:], in_=z[:])
            if width == HALF:
                banks = [psum.tile([P, S], F32, name="h_acc%d_%d" % (n, t), tag="bank%d" % t)[:, 0:width] for t in range(PACK)]
            else:
                shared = [psum.tile([P, S], F32, name="h_acc%d_%d" % (n, u), tag="bank%d" % (2 + 2 * n + u)) for u in range(2)]
                banks = [shared[t // 2][:, (t % 2) * width : (t % 2 + 1) * width] for t in range(PACK)]
            for t in range(PACK):
                nc.tensor.matmul_mx(
                    out=banks[t],
                    lhsT=w_dealt[:, 2 * t * P : 2 * (t + 1) * P].bitcast(FP4X4),
                    lhsT_scale=w_sc[:, t * P : (t + 1) * P],
                    rhs=z_w[:].bitcast(FP8X4),
                    rhs_scale=z_sc[:],
                    start=True,
                    stop=True,
                )
            done = half(span.start // HALF)
            for t in range(PACK):
                nc.scalar.activation(h_abs[t][:, span], banks[t], ACT.Abs)
                if span.stop == done.stop and (n, t) != (0, 0):
                    nc.sync.dma_start(abs_copy[t][:, done], h_abs[t][:, done])
            if n == 0:
                nc.scalar.copy(abs_copy[0][:, done], h_abs[0][:, done])
            h_acc.append(banks)
        for n, span in enumerate(stretches):
            copy = nc.scalar.copy if span.stop == S else nc.vector.tensor_copy
            for t in range(PACK):
                copy(h_val[t][:, span], h_acc[n][t])

        h_far = sb.tile([P, PACK - H_FUSED_TILES, HALF], F32, name="h_far")
        for t in range(H_FUSED_TILES, PACK):
            nc.scalar.activation(h_far[:, t - H_FUSED_TILES, :], h_val[t][:].indirect(entries(n3_l, half(1))), ACT.Copy)
        den = sb.tile([P, PACK, S], F32, name="den")
        for h in range(2):
            for t in range(PACK):
                nc.vector.tensor_tensor(den[:, t, half(h)], h_abs[t][:].indirect(entries(n4_l, half(h))), abs_copy[t][:, half(h)], ALU.add)
        inv = sb.tile([P, PACK, S], F32, name="inv")
        for h in range(2):
            for t in range(PACK):
                root = sb.tile([P, HALF], F32, name="root%d_%d" % (h, t), tag="root%d_%d" % (h, t), align_bytes=ALIGN)
                nc.scalar.activation(root[:], den[:, t, half(h)], ACT.Abs_reciprocal_sqrt, bias=one_half[:])
                nc.scalar.activation(inv[:, t, half(h)], root[:], ACT.Square)

        out_rows = out_0.rearrange("(p t) j -> p t j", t=PACK)
        out_words = out_1[0].rearrange("p n r -> p (n r)").bitcast(I32)
        o_w = sb.tile([P, S], U32, name="o_w", align_bytes=ALIGN)
        o_sc = sb.tile([P, S], U8, name="o_sc", align_bytes=ALIGN)
        res = [sb.tile([P, PACK, HALF], F32, name="res%d" % h, tag=("h_abs3", "res1")[h], align_bytes=ALIGN) for h in range(2)]
        res_bf = [sb.tile([P, HALF * PACK], BF16, name="res_bf%d" % h, tag=("root1_2", "res_bf1")[h], align_bytes=ALIGN) for h in range(2)]
        for h in range(2):
            fused = PACK if h == 0 else H_FUSED_TILES
            for t in range(fused):
                nc.vector.tensor_tensor(res[h][:, t, :], h_val[t][:].indirect(entries(n3_l, half(h))), inv[:, t, half(h)], ALU.mult)
            if fused < PACK:
                nc.vector.tensor_tensor(res[h][:, fused:PACK, :], h_far[:], inv[:, fused:PACK, half(h)], ALU.mult)
            for t in range(0, PACK, 2):
                nc.sync.dma_start(out_rows[:, t : t + 2, half(h)], res[h][:, t : t + 2, :])
            cut = HALF if h == 0 else ROUND_ON_SCALAR
            nc.scalar.copy(side_by_side(res_bf[h][:, 0 : PACK * cut]), by_pairs(res[h][:, :, 0:cut]))
            if cut < HALF:
                nc.vector.tensor_copy(side_by_side(res_bf[h][:, PACK * cut :]), by_pairs(res[h][:, :, cut:]))
            nc.vector.quantize_mx(out=o_w[:, half(h)].bitcast(FP8X4), scales=o_sc[:, half(h)], in_=res_bf[h][:])
            nc.sync.dma_start(out_words[:, half(h)], o_w[:, half(h)].bitcast(I32))
        for q in range(4):
            queue = nc.sync if q == 0 else nc.scalar
            queue.dma_start(out_2[0, 4 * q : 4 * q + 4, :].bitcast(I32), o_sc[32 * q : 32 * q + 4, :].bitcast(I32))
